import numpy as np
import ml_dtypes

BF16 = ml_dtypes.bfloat16


def bf(x):
    return np.asarray(x, np.float32).astype(BF16)


def f32(x):
    return np.asarray(x, np.float32)


def f64(x):
    return np.asarray(x).astype(np.float64)


def striped(idx):
    return np.tile(idx.reshape(-1, 16).T, (8, 1))


S, K, M, N, E, Q = 256, 128, 256, 192, 2, 96


def setup_inputs():
    return {"base": bf(np.random.standard_normal((M, S))), "x": bf(np.random.standard_normal((K, N))), "w": bf(np.random.standard_normal((E, K, M)) / np.sqrt(K)), "b": f32(0.5 * np.random.standard_normal((M, 1))), "offs": striped(np.random.permutation(S)[:N])}


def reference(base, x, w, b, offs):
    idx = offs[:16].T.reshape(-1)
    z = f64(base).copy()
    for e in range(E):
        z[:, idx[e * Q : (e + 1) * Q]] = f64(w)[e].T @ f64(x)[:, e * Q : (e + 1) * Q]
    return np.maximum(z + f64(b), 0.0)

@@ -1,0 +1,64 @@
+import concourse.mybir as mybir
+from concourse.masks import make_identity
+
+BF16 = mybir.dt.bfloat16
+F32 = mybir.dt.float32
+U16 = mybir.dt.uint16
+
+P = 128
+TOKENS = 256
+ENTRIES = 192
+EXPERTS = 2
+PIECE = ENTRIES // EXPERTS
+PIECE_COLS = PIECE // 16
+BLOCKS = 2
+
+FLOPS = 2 * P * (BLOCKS * P) * ENTRIES
+
+
+def tile_scatter_matmul_kernel(tc, base, x, w, b, offs, out):
+    nc = tc.nc
+    with (
+        tc.tile_pool(name="held", bufs=1) as held,
+        tc.psum_pool(name="windows", bufs=1) as windows,
+    ):
+        offsets = held.tile([P, ENTRIES // 16], U16, name="offsets")
+        nc.sync.dma_start(offsets[:], offs)
+        base_sb = held.tile([P, BLOCKS, TOKENS], BF16, name="base_sb")
+        nc.scalar.dma_start(base_sb[:], base.rearrange("(a p) t -> p a t", p=P))
+        x_sb = held.tile([P, ENTRIES], BF16, name="x_sb")
+        nc.sync.dma_start(x_sb[:], x)
+        w_sb = held.tile([P, EXPERTS, BLOCKS * P], BF16, name="w_sb")
+        nc.scalar.dma_start(w_sb[:], w.rearrange("e k m -> k e m"))
+        bias = held.tile([P, BLOCKS], F32, name="bias")
+        with nc.allow_non_contiguous_dma(reason="256 bias values, one to a partition"):
+            nc.sync.dma_start(bias[:], b.rearrange("(a p) o -> p (a o)", p=P))
+
+        ident = held.tile([P, P], BF16, name="ident")
+        make_identity(nc, ident[:])
+
+        window = [windows.tile([P, TOKENS], F32, name="window%d" % a) for a in range(BLOCKS)]
+        for a in range(BLOCKS):
+            nc.tensor.matmul(window[a][:], ident[:], base_sb[:, a, :], start=True, stop=True)
+
+        for a in range(BLOCKS):
+            for e in range(EXPERTS):
+                nc.tensor.matmul(
+                    window[a][:].indirect(offsets[:, e * PIECE_COLS : (e + 1) * PIECE_COLS]),
+                    w_sb[:, e, a * P : (a + 1) * P],
+                    x_sb[:, e * PIECE : (e + 1) * PIECE],
+                    start=True,
+                    stop=True,
+                )
+
+        result0 = held.tile([P, TOKENS], F32, name="result0")
+        nc.vector.tensor_scalar(
+            result0[:], window[0][:], bias[:, 0:1], 0.0,
+            op0=mybir.AluOpType.add, op1=mybir.AluOpType.max,
+        )
+        nc.sync.dma_start(out[0:P, :], result0[:])
+        result1 = held.tile([P, TOKENS], F32, name="result1")
+        nc.scalar.activation(
+            result1[:], window[1][:], mybir.ActivationFunctionType.Relu, bias=bias[:, 1:2],
+        )
+        nc.scalar.dma_start(out[P : 2 * P, :], result1[:])

@@ -51,14 +51,11 @@ def tile_scatter_matmul_kernel(tc, base, x, w, b, offs, out):
                     stop=True,
                 )
 
-        result0 = held.tile([P, TOKENS], F32, name="result0")
-        nc.vector.tensor_scalar(
-            result0[:], window[0][:], bias[:, 0:1], 0.0,
-            op0=mybir.AluOpType.add, op1=mybir.AluOpType.max,
-        )
-        nc.sync.dma_start(out[0:P, :], result0[:])
-        result1 = held.tile([P, TOKENS], F32, name="result1")
-        nc.scalar.activation(
-            result1[:], window[1][:], mybir.ActivationFunctionType.Relu, bias=bias[:, 1:2],
-        )
-        nc.scalar.dma_start(out[P : 2 * P, :], result1[:])
+        stores = [nc.sync, nc.scalar]
+        for a in range(BLOCKS):
+            result = held.tile([P, TOKENS], F32, name="result%d" % a)
+            nc.vector.tensor_scalar(
+                result[:], window[a][:], bias[:, a : a + 1], 0.0,
+                op0=mybir.AluOpType.add, op1=mybir.AluOpType.max,
+            )
+            stores[a].dma_start(out[a * P : (a + 1) * P, :], result[:])

@@ -22,14 +22,15 @@ def tile_scatter_matmul_kernel(tc, base, x, w, b, offs, out):
         tc.tile_pool(name="held", bufs=1) as held,
         tc.psum_pool(name="windows", bufs=1) as windows,
     ):
+        base_sb = [held.tile([P, TOKENS], BF16, name="base_sb%d" % a) for a in range(BLOCKS)]
+        nc.sync.dma_start(base_sb[0][:], base[0:P, :])
+        nc.scalar.dma_start(base_sb[1][:], base[P : 2 * P, :])
         offsets = held.tile([P, ENTRIES // 16], U16, name="offsets")
         nc.sync.dma_start(offsets[:], offs)
-        base_sb = held.tile([P, BLOCKS, TOKENS], BF16, name="base_sb")
-        nc.scalar.dma_start(base_sb[:], base.rearrange("(a p) t -> p a t", p=P))
-        x_sb = held.tile([P, ENTRIES], BF16, name="x_sb")
-        nc.sync.dma_start(x_sb[:], x)
         w_sb = held.tile([P, EXPERTS, BLOCKS * P], BF16, name="w_sb")
         nc.scalar.dma_start(w_sb[:], w.rearrange("e k m -> k e m"))
+        x_sb = held.tile([P, ENTRIES], BF16, name="x_sb")
+        nc.sync.dma_start(x_sb[:], x)
         bias = held.tile([P, BLOCKS], F32, name="bias")
         with nc.allow_non_contiguous_dma(reason="256 bias values, one to a partition"):
             nc.sync.dma_start(bias[:], b.rearrange("(a p) o -> p (a o)", p=P))
@@ -39,7 +40,7 @@ def tile_scatter_matmul_kernel(tc, base, x, w, b, offs, out):
 
         window = [windows.tile([P, TOKENS], F32, name="window%d" % a) for a in range(BLOCKS)]
         for a in range(BLOCKS):
-            nc.tensor.matmul(window[a][:], ident[:], base_sb[:, a, :], start=True, stop=True)
+            nc.tensor.matmul(window[a][:], ident[:], base_sb[a][:], start=True, stop=True)
 
         for a in range(BLOCKS):
             for e in range(EXPERTS):

@@ -13,6 +13,9 @@ PIECE = ENTRIES // EXPERTS
 PIECE_COLS = PIECE // 16
 BLOCKS = 2
 
+WARM_COLS = 512
+WARM_MATMULS = 3
+
 FLOPS = 2 * P * (BLOCKS * P) * ENTRIES
 
 
@@ -22,25 +25,30 @@ def tile_scatter_matmul_kernel(tc, base, x, w, b, offs, out):
         tc.tile_pool(name="held", bufs=1) as held,
         tc.psum_pool(name="windows", bufs=1) as windows,
     ):
-        base_sb = [held.tile([P, TOKENS], BF16, name="base_sb%d" % a) for a in range(BLOCKS)]
-        nc.sync.dma_start(base_sb[0][:], base[0:P, :])
-        nc.scalar.dma_start(base_sb[1][:], base[P : 2 * P, :])
         offsets = held.tile([P, ENTRIES // 16], U16, name="offsets")
         nc.sync.dma_start(offsets[:], offs)
-        w_sb = held.tile([P, EXPERTS, BLOCKS * P], BF16, name="w_sb")
-        nc.scalar.dma_start(w_sb[:], w.rearrange("e k m -> k e m"))
+        base_sb = held.tile([P, BLOCKS, TOKENS], BF16, name="base_sb")
+        nc.scalar.dma_start(base_sb[:], base.rearrange("(a p) t -> p a t", p=P))
         x_sb = held.tile([P, ENTRIES], BF16, name="x_sb")
         nc.sync.dma_start(x_sb[:], x)
+        w_sb = held.tile([P, EXPERTS, BLOCKS * P], BF16, name="w_sb")
+        nc.scalar.dma_start(w_sb[:], w.rearrange("e k m -> k e m"))
         bias = held.tile([P, BLOCKS], F32, name="bias")
         with nc.allow_non_contiguous_dma(reason="256 bias values, one to a partition"):
             nc.sync.dma_start(bias[:], b.rearrange("(a p) o -> p (a o)", p=P))
+
+        zeros = held.tile([P, WARM_COLS], BF16, name="zeros")
+        nc.vector.memset(zeros[:], 0.0)
+        unread = windows.tile([P, WARM_COLS], F32, name="unread")
+        for i in range(WARM_MATMULS):
+            nc.tensor.matmul(unread[:], zeros[:, 0:P], zeros[:], start=True, stop=True)
 
         ident = held.tile([P, P], BF16, name="ident")
         make_identity(nc, ident[:])
 
         window = [windows.tile([P, TOKENS], F32, name="window%d" % a) for a in range(BLOCKS)]
         for a in range(BLOCKS):
-            nc.tensor.matmul(window[a][:], ident[:], base_sb[a][:], start=True, stop=True)
+            nc.tensor.matmul(window[a][:], ident[:], base_sb[:, a, :], start=True, stop=True)
 
         for a in range(BLOCKS):
             for e in range(EXPERTS):

@@ -33,9 +33,9 @@ def tile_scatter_matmul_kernel(tc, base, x, w, b, offs, out):
         nc.sync.dma_start(x_sb[:], x)
         w_sb = held.tile([P, EXPERTS, BLOCKS * P], BF16, name="w_sb")
         nc.scalar.dma_start(w_sb[:], w.rearrange("e k m -> k e m"))
-        bias = held.tile([P, BLOCKS], F32, name="bias")
-        with nc.allow_non_contiguous_dma(reason="256 bias values, one to a partition"):
-            nc.sync.dma_start(bias[:], b.rearrange("(a p) o -> p (a o)", p=P))
+        bias = [held.tile([P, 1], F32, name="bias%d" % a) for a in range(BLOCKS)]
+        nc.sync.dma_start(bias[0][:], b[0:P, :])
+        nc.scalar.dma_start(bias[1][:], b[P : 2 * P, :])
 
         zeros = held.tile([P, WARM_COLS], BF16, name="zeros")
         nc.vector.memset(zeros[:], 0.0)
@@ -64,7 +64,7 @@ def tile_scatter_matmul_kernel(tc, base, x, w, b, offs, out):
         for a in range(BLOCKS):
             result = held.tile([P, TOKENS], F32, name="result%d" % a)
             nc.vector.tensor_scalar(
-                result[:], window[a][:], bias[:, a : a + 1], 0.0,
+                result[:], window[a][:], bias[a][:], 0.0,
                 op0=mybir.AluOpType.add, op1=mybir.AluOpType.max,
             )
             stores[a].dma_start(out[a * P : (a + 1) * P, :], result[:])

@@ -13,8 +13,8 @@ PIECE = ENTRIES // EXPERTS
 PIECE_COLS = PIECE // 16
 BLOCKS = 2
 
-WARM_COLS = 512
-WARM_MATMULS = 3
+WARM_COLS = P
+WARM_MATMULS = 12
 
 FLOPS = 2 * P * (BLOCKS * P) * ENTRIES
 
@@ -41,7 +41,7 @@ def tile_scatter_matmul_kernel(tc, base, x, w, b, offs, out):
         nc.vector.memset(zeros[:], 0.0)
         unread = windows.tile([P, WARM_COLS], F32, name="unread")
         for i in range(WARM_MATMULS):
-            nc.tensor.matmul(unread[:], zeros[:, 0:P], zeros[:], start=True, stop=True)
+            nc.tensor.matmul(unread[:], zeros[:], zeros[:], start=True, stop=True)
 
         ident = held.tile([P, P], BF16, name="ident")
         make_identity(nc, ident[:])

@@ -11,6 +11,7 @@ ENTRIES = 192
 EXPERTS = 2
 PIECE = ENTRIES // EXPERTS
 PIECE_COLS = PIECE // 16
+ROW_ALIGN = 256
 BLOCKS = 2
 
 WARM_COLS = P
@@ -27,11 +28,11 @@ def tile_scatter_matmul_kernel(tc, base, x, w, b, offs, out):
     ):
         offsets = held.tile([P, ENTRIES // 16], U16, name="offsets")
         nc.sync.dma_start(offsets[:], offs)
-        base_sb = held.tile([P, BLOCKS, TOKENS], BF16, name="base_sb")
+        base_sb = held.tile([P, BLOCKS, TOKENS], BF16, name="base_sb", align_bytes=ROW_ALIGN)
         nc.scalar.dma_start(base_sb[:], base.rearrange("(a p) t -> p a t", p=P))
-        x_sb = held.tile([P, ENTRIES], BF16, name="x_sb")
+        x_sb = held.tile([P, ENTRIES], BF16, name="x_sb", align_bytes=ROW_ALIGN)
         nc.sync.dma_start(x_sb[:], x)
-        w_sb = held.tile([P, EXPERTS, BLOCKS * P], BF16, name="w_sb")
+        w_sb = held.tile([P, EXPERTS, BLOCKS * P], BF16, name="w_sb", align_bytes=ROW_ALIGN)
         nc.scalar.dma_start(w_sb[:], w.rearrange("e k m -> k e m"))
         bias = [held.tile([P, 1], F32, name="bias%d" % a) for a in range(BLOCKS)]
         nc.sync.dma_start(bias[0][:], b[0:P, :])
@@ -62,7 +63,7 @@ def tile_scatter_matmul_kernel(tc, base, x, w, b, offs, out):
 
         stores = [nc.sync, nc.scalar]
         for a in range(BLOCKS):
-            result = held.tile([P, TOKENS], F32, name="result%d" % a)
+            result = held.tile([P, TOKENS], F32, name="result%d" % a, align_bytes=ROW_ALIGN)
             nc.vector.tensor_scalar(
                 result[:], window[a][:], bias[a][:], 0.0,
                 op0=mybir.AluOpType.add, op1=mybir.AluOpType.max,

@@ -29,14 +29,13 @@ def tile_scatter_matmul_kernel(tc, base, x, w, b, offs, out):
         offsets = held.tile([P, ENTRIES // 16], U16, name="offsets")
         nc.sync.dma_start(offsets[:], offs)
         base_sb = held.tile([P, BLOCKS, TOKENS], BF16, name="base_sb", align_bytes=ROW_ALIGN)
-        nc.scalar.dma_start(base_sb[:], base.rearrange("(a p) t -> p a t", p=P))
+        nc.scalar.dma_start(base_sb[:], base.rearrange("(p a) t -> p a t", a=BLOCKS))
         x_sb = held.tile([P, ENTRIES], BF16, name="x_sb", align_bytes=ROW_ALIGN)
         nc.sync.dma_start(x_sb[:], x)
         w_sb = held.tile([P, EXPERTS, BLOCKS * P], BF16, name="w_sb", align_bytes=ROW_ALIGN)
         nc.scalar.dma_start(w_sb[:], w.rearrange("e k m -> k e m"))
-        bias = [held.tile([P, 1], F32, name="bias%d" % a) for a in range(BLOCKS)]
-        nc.sync.dma_start(bias[0][:], b[0:P, :])
-        nc.scalar.dma_start(bias[1][:], b[P : 2 * P, :])
+        bias = held.tile([P, BLOCKS], F32, name="bias")
+        nc.sync.dma_start(bias[:], b.rearrange("(p a) o -> p (a o)", a=BLOCKS))
 
         zeros = held.tile([P, WARM_COLS], BF16, name="zeros")
         nc.vector.memset(zeros[:], 0.0)
@@ -55,17 +54,18 @@ def tile_scatter_matmul_kernel(tc, base, x, w, b, offs, out):
             for e in range(EXPERTS):
                 nc.tensor.matmul(
                     window[a][:].indirect(offsets[:, e * PIECE_COLS : (e + 1) * PIECE_COLS]),
-                    w_sb[:, e, a * P : (a + 1) * P],
+                    w_sb[:, e, a::BLOCKS],
                     x_sb[:, e * PIECE : (e + 1) * PIECE],
                     start=True,
                     stop=True,
                 )
 
         stores = [nc.sync, nc.scalar]
+        out_blocks = out.rearrange("(p a) t -> p a t", a=BLOCKS)
         for a in range(BLOCKS):
             result = held.tile([P, TOKENS], F32, name="result%d" % a, align_bytes=ROW_ALIGN)
             nc.vector.tensor_scalar(
-                result[:], window[a][:], bias[a][:], 0.0,
+                result[:], window[a][:], bias[:, a : a + 1], 0.0,
                 op0=mybir.AluOpType.add, op1=mybir.AluOpType.max,
             )
-            stores[a].dma_start(out[a * P : (a + 1) * P, :], result[:])
+            stores[a].dma_start(out_blocks[:, a, :], result[:])

@@ -61,11 +61,15 @@ def tile_scatter_matmul_kernel(tc, base, x, w, b, offs, out):
                 )
 
         stores = [nc.sync, nc.scalar]
+        parts = [1, 2]
         out_blocks = out.rearrange("(p a) t -> p a t", a=BLOCKS)
         for a in range(BLOCKS):
-            result = held.tile([P, TOKENS], F32, name="result%d" % a, align_bytes=ROW_ALIGN)
-            nc.vector.tensor_scalar(
-                result[:], window[a][:], bias[:, a : a + 1], 0.0,
-                op0=mybir.AluOpType.add, op1=mybir.AluOpType.max,
-            )
-            stores[a].dma_start(out_blocks[:, a, :], result[:])
+            width = TOKENS // parts[a]
+            for h in range(parts[a]):
+                columns = slice(h * width, (h + 1) * width)
+                result = held.tile([P, width], F32, name="result%d_%d" % (a, h), align_bytes=ROW_ALIGN)
+                nc.vector.tensor_scalar(
+                    result[:], window[a][:, columns], bias[:, a : a + 1], 0.0,
+                    op0=mybir.AluOpType.add, op1=mybir.AluOpType.max,
+                )
+                stores[a].dma_start(out_blocks[:, a, columns], result[:])

@@ -37,18 +37,18 @@ def tile_scatter_matmul_kernel(tc, base, x, w, b, offs, out):
         bias = held.tile([P, BLOCKS], F32, name="bias")
         nc.sync.dma_start(bias[:], b.rearrange("(p a) o -> p (a o)", a=BLOCKS))
 
-        zeros = held.tile([P, WARM_COLS], BF16, name="zeros")
-        nc.vector.memset(zeros[:], 0.0)
+        cleared = held.tile([P, P + WARM_COLS], BF16, name="cleared")
+        nc.vector.memset(cleared[:], 0.0)
+        ident = cleared[:, 0:P]
+        zeros = cleared[:, P : P + WARM_COLS]
+        make_identity(nc, ident, nomemset=True)
         unread = windows.tile([P, WARM_COLS], F32, name="unread")
         for i in range(WARM_MATMULS):
-            nc.tensor.matmul(unread[:], zeros[:], zeros[:], start=True, stop=True)
-
-        ident = held.tile([P, P], BF16, name="ident")
-        make_identity(nc, ident[:])
+            nc.tensor.matmul(unread[:], zeros, zeros, start=True, stop=True)
 
         window = [windows.tile([P, TOKENS], F32, name="window%d" % a) for a in range(BLOCKS)]
         for a in range(BLOCKS):
-            nc.tensor.matmul(window[a][:], ident[:], base_sb[:, a, :], start=True, stop=True)
+            nc.tensor.matmul(window[a][:], ident, base_sb[:, a, :], start=True, stop=True)
 
         for a in range(BLOCKS):
             for e in range(EXPERTS):

import concourse.mybir as mybir
from concourse.masks import make_identity

BF16 = mybir.dt.bfloat16
F32 = mybir.dt.float32
U16 = mybir.dt.uint16

P = 128
TOKENS = 256
ENTRIES = 192
EXPERTS = 2
PIECE = ENTRIES // EXPERTS
PIECE_COLS = PIECE // 16
ROW_ALIGN = 256
BLOCKS = 2

WARM_COLS = P
WARM_MATMULS = 12

FLOPS = 2 * P * (BLOCKS * P) * ENTRIES


def tile_scatter_matmul_kernel(tc, base, x, w, b, offs, out):
    nc = tc.nc
    with (
        tc.tile_pool(name="held", bufs=1) as held,
        tc.psum_pool(name="windows", bufs=1) as windows,
    ):
        offsets = held.tile([P, ENTRIES // 16], U16, name="offsets")
        nc.sync.dma_start(offsets[:], offs)
        base_sb = held.tile([P, BLOCKS, TOKENS], BF16, name="base_sb", align_bytes=ROW_ALIGN)
        nc.scalar.dma_start(base_sb[:], base.rearrange("(p a) t -> p a t", a=BLOCKS))
        x_sb = held.tile([P, ENTRIES], BF16, name="x_sb", align_bytes=ROW_ALIGN)
        nc.sync.dma_start(x_sb[:], x)
        w_sb = held.tile([P, EXPERTS, BLOCKS * P], BF16, name="w_sb", align_bytes=ROW_ALIGN)
        nc.scalar.dma_start(w_sb[:], w.rearrange("e k m -> k e m"))
        bias = held.tile([P, BLOCKS], F32, name="bias")
        nc.sync.dma_start(bias[:], b.rearrange("(p a) o -> p (a o)", a=BLOCKS))

        cleared = held.tile([P, P + WARM_COLS], BF16, name="cleared")
        nc.vector.memset(cleared[:], 0.0)
        ident = cleared[:, 0:P]
        zeros = cleared[:, P : P + WARM_COLS]
        make_identity(nc, ident, nomemset=True)
        unread = windows.tile([P, WARM_COLS], F32, name="unread")
        for i in range(WARM_MATMULS):
            nc.tensor.matmul(unread[:], zeros, zeros, start=True, stop=True)

        window = [windows.tile([P, TOKENS], F32, name="window%d" % a) for a in range(BLOCKS)]
        for a in range(BLOCKS):
            nc.tensor.matmul(window[a][:], ident, base_sb[:, a, :], start=True, stop=True)

        for a in range(BLOCKS):
            for e in range(EXPERTS):
                nc.tensor.matmul(
                    window[a][:].indirect(offsets[:, e * PIECE_COLS : (e + 1) * PIECE_COLS]),
                    w_sb[:, e, a::BLOCKS],
                    x_sb[:, e * PIECE : (e + 1) * PIECE],
                    start=True,
                    stop=True,
                )

        stores = [nc.sync, nc.scalar]
        parts = [1, 2]
        out_blocks = out.rearrange("(p a) t -> p a t", a=BLOCKS)
        for a in range(BLOCKS):
            width = TOKENS // parts[a]
            for h in range(parts[a]):
                columns = slice(h * width, (h + 1) * width)
                result = held.tile([P, width], F32, name="result%d_%d" % (a, h), align_bytes=ROW_ALIGN)
                nc.vector.tensor_scalar(
                    result[:], window[a][:, columns], bias[:, a : a + 1], 0.0,
                    op0=mybir.AluOpType.add, op1=mybir.AluOpType.max,
                )
                stores[a].dma_start(out_blocks[:, a, columns], result[:])
